import numpy as np
import ml_dtypes


def mxq(x, axis, fmt="e4m3"):
    dtype, down = {"e4m3": (ml_dtypes.float8_e4m3fn, 7), "e5m2": (ml_dtypes.float8_e5m2, 14)}[fmt]
    v = np.moveaxis(np.asarray(x, np.float32).astype(ml_dtypes.bfloat16).astype(np.float64), axis, -1)
    blocks = v.reshape(v.shape[:-1] + (-1, 32))
    amax = np.abs(blocks).max(-1, keepdims=True)
    byte = np.maximum(np.where(amax > 0, np.frexp(amax)[1] - 1 + 127, 0) - down, 1)
    scale = np.exp2(byte - 127.0)
    codes = (blocks / scale).astype(np.float32).astype(dtype).astype(np.float64)
    return np.moveaxis((codes * scale).reshape(v.shape), -1, axis)


WIDE = False


def mx_kscale(k):
    if not WIDE:
        return np.ones(k)
    levels = np.array([10, -10, 5, -5, 0])
    if k % 512:
        return np.exp2(np.random.permutation(np.resize(levels, k // 32))).repeat(32)
    a = np.empty((k // 512, 16))
    for p in range(k // 512):
        a[p, :8] = np.random.permutation(np.resize(levels, 8))
        for g in range(8):
            far = levels[np.abs(levels - a[p, g]) >= 10]
            a[p, g + 8] = far[np.random.randint(len(far))]
    return np.exp2(a.ravel()).repeat(32)


def f64(x):
    return np.asarray(x).astype(np.float64)


def striped(idx):
    return np.tile(idx.reshape(-1, 16).T, (8, 1)).astype(np.uint16)


def unstriped(offs):
    return offs[:16].T.reshape(-1).astype(np.int64)


E2M1 = np.array([0.0, 0.5, 1.0, 1.5, 2.0, 3.0, 4.0, 6.0, -0.0, -0.5, -1.0, -1.5, -2.0, -3.0, -4.0, -6.0])


def pack_weight(w, fmt):
    k, n = w.shape
    w = f64(np.asarray(w, np.float32).astype(ml_dtypes.bfloat16)).reshape(k // 32, 32, n)
    amax = np.abs(w).max(1)
    if fmt == "e4m3":
        byte = np.frexp(amax)[1] - 1 + 127 - 7
    else:
        mant, ex = np.frexp(amax / 6.0)
        byte = np.where(mant > 0.5, ex, ex - 1) + 127
    byte = np.clip(np.where(amax > 0, byte, 1), 1, 254)
    scaled = (w * np.exp2(127.0 - byte)[:, None, :]).reshape(k, n).astype(np.float32)
    by_word = np.ascontiguousarray(scaled.reshape(k // 512, 128, 4, n).transpose(0, 1, 3, 2))
    if fmt == "e4m3":
        words = by_word.astype(ml_dtypes.float8_e4m3fn).view(np.uint8)
    else:
        c = by_word.astype(ml_dtypes.float4_e2m1fn).view(np.uint8) & 0xF
        words = (c[..., 0::2] | (c[..., 1::2] << 4)).reshape(k // 512, 128, 2 * n)
    return np.ascontiguousarray(words), np.ascontiguousarray(byte.astype(np.uint8).reshape(k // 512, 16, n))


def unpack_weight(words, scales, fmt):
    g, _, n = scales.shape
    words = np.ascontiguousarray(words).reshape(g, 128, n, -1)
    if fmt == "e4m3":
        vals = words.view(ml_dtypes.float8_e4m3fn).astype(np.float64)
    else:
        nib = np.empty((g, 128, n, 4), np.uint8)
        nib[..., 0::2] = words & 0xF
        nib[..., 1::2] = words >> 4
        vals = E2M1[nib]
    vals = vals * np.repeat(np.exp2(scales.astype(np.float64) - 127.0), 8, axis=1)[..., None]
    return vals.transpose(0, 1, 3, 2).reshape(g * 512, n)


def gelu(v):
    return 0.5 * v * (1.0 + np.tanh(np.sqrt(2.0 / np.pi) * (v + 0.044715 * v**3)))


K, H, T, S, T2, P, T3, S2 = 1024, 1024, 4096, 1024, 2048, 512, 2048, 1024


def setup_inputs():
    n = np.random.standard_normal
    s = mx_kscale(K)[:, None]
    u = mx_kscale(H)[:, None]
    tab_words, tab_scales = pack_weight(n((K, T)) * s, "e4m3")
    tab2_words, tab2_scales = pack_weight(n((H, T3)) / np.sqrt(H) / u, "e4m3")
    sk_words, sk_scales = pack_weight(n((H, P)) * u, "e2m1")
    return {
        "tab_words": tab_words, "tab_scales": tab_scales,
        "offs": striped(np.random.permutation(T)[:S]),
        "w1": (n((K, H)) / np.sqrt(K) / s * u.T).astype(np.float32),
        "chain": (0.7 * n((H, S)) * u).astype(np.float32),
        "page0": (n((H, T2)) * u).astype(np.float32),
        "wgs": np.exp(0.3 * n((128, S))).astype(np.float32),
        "offs3": striped(np.random.permutation(T2)[:S]),
        "offs4": striped(np.random.permutation(T2)[:P]),
        "gain": np.exp(0.4 * n(H)).astype(np.float32),
        "tab2_words": tab2_words, "tab2_scales": tab2_scales,
        "offs2": striped(np.random.permutation(T3)[:S2]),
        "sk_words": sk_words, "sk_scales": sk_scales,
        "period": np.exp(0.4 * n((S2, P))).astype(np.float32),
    }


def reference(tab_words, tab_scales, offs, w1, chain, page0, wgs, offs3, offs4, gain,
              tab2_words, tab2_scales, offs2, sk_words, sk_scales, period):
    v = unpack_weight(tab_words, tab_scales, "e4m3")[:, unstriped(offs)]
    h = (mxq(f64(w1), 0, "e4m3").T @ v) + f64(chain)
    page = f64(page0).copy()
    page[:, unstriped(offs3)] = np.tile(f64(wgs), (H // 128, 1)) * h
    x = page[:, unstriped(offs4)] * f64(gain)[:, None]
    xq = mxq(x, 0, "e4m3")
    v2 = unpack_weight(tab2_words, tab2_scales, "e4m3")[:, unstriped(offs2)]
    sk = unpack_weight(sk_words, sk_scales, "e2m1")
    e = v2.T @ xq
    q = v2.T @ sk
    return np.maximum(np.tanh(e) * f64(period), q)

@@ -1,0 +1,333 @@
+from contextlib import ExitStack
+
+import concourse.mybir as mybir
+from concourse.masks import make_identity
+
+K, H, T, S, T2, NP, T3, S2 = 1024, 1024, 4096, 1024, 2048, 512, 2048, 1024
+FLOPS = 2 * K * H * S + 2 * 2 * H * S2 * NP
+
+F32 = mybir.dt.float32
+BF16 = mybir.dt.bfloat16
+I32 = mybir.dt.int32
+U32 = mybir.dt.uint32
+U16 = mybir.dt.uint16
+U8 = mybir.dt.uint8
+FP8X4 = mybir.dt.float8_e4m3fn_x4
+FP4X4 = mybir.dt.float4_e2m1fn_x4
+MULT = mybir.AluOpType.mult
+ADD = mybir.AluOpType.add
+MAX = mybir.AluOpType.max
+COPY = mybir.ActivationFunctionType.Copy
+TANH = mybir.ActivationFunctionType.Tanh
+
+P = 128
+BANK = 512
+
+
+def tile_list_watermark_candidate_scores_kernel(
+    tc, tab_words, tab_scales, offs, w1, chain, page0, wgs, offs3, offs4, gain,
+    tab2_words, tab2_scales, offs2, sk_words, sk_scales, period, out,
+):
+    nc = tc.nc
+    with ExitStack() as ctx:
+        lists = ctx.enter_context(tc.tile_pool(name="lists", bufs=1))
+        keep = ctx.enter_context(tc.tile_pool(name="keep", bufs=1))
+        two = ctx.enter_context(tc.tile_pool(name="two", bufs=2))
+        three = ctx.enter_context(tc.tile_pool(name="three", bufs=3))
+        psum = ctx.enter_context(tc.psum_pool(name="psum", bufs=1))
+
+        def bank(b):
+            return psum.tile([P, BANK], F32, name=f"bank{b}", tag=f"bank{b}")
+
+        def load_list(src, name):
+            tile = lists.tile(list(src.shape), U16, name=name)
+            nc.sync.dma_start(tile[:], src)
+            return tile
+
+        chain_rows = chain.rearrange("(a p t) j -> a t p j", a=2, t=4)
+        page_rows = page0.rearrange("(a p t) c -> a t p c", a=2, t=4)
+        wgs_rows = wgs.rearrange("(q t) j -> q t j", t=4)
+
+        tab_sc = keep.tile([P, T], U8, name="tab_sc", align_bytes=64)
+        nc.vector.memset(tab_sc[:].bitcast(I32), 0)
+        tab2_sc = keep.tile([P, 2, T3], U8, name="tab2_sc", align_bytes=64)
+        nc.vector.memset(tab2_sc[:].bitcast(I32), 0)
+        sk_sc = keep.tile([P, 2, NP], U8, name="sk_sc", align_bytes=64)
+        nc.gpsimd.memset(sk_sc[:].bitcast(I32), 0)
+        ident = keep.tile([P, P], F32, name="ident")
+        make_identity(nc, ident[:])
+
+        w_codes = {}
+        w_scales = {}
+
+        def load_w1(a, b):
+            raw = two.tile([P, 4, BANK], F32, name="w_raw", tag="w_raw")
+            rows = w1[512 * a : 512 * (a + 1), 512 * b : 512 * (b + 1)]
+            nc.sync.dma_start(raw[:], rows.rearrange("(p j) c -> p j c", j=4))
+            return raw
+
+        def quantise_w1(a, b, raw, codes):
+            grouped = two.tile([P, 4 * BANK], BF16, name="w_grouped", tag="w_grouped", align_bytes=64)
+            nc.scalar.copy(
+                grouped[:].rearrange("p (t m j) -> p m t j", t=4, j=4),
+                raw[:].rearrange("p j (m t) -> p m t j", t=4),
+            )
+            w_codes[a, b] = codes
+            w_scales[a, b] = keep.tile([P, BANK], U8, name=f"w_scales{a}{b}", align_bytes=64)
+            nc.vector.quantize_mx(codes.bitcast(FP8X4), w_scales[a, b][:], grouped[:])
+
+        def load_chain(i):
+            tile = three.tile([P, S], F32, name="chain", tag="chain")
+            nc.sync.dma_start(tile[:], chain_rows[i // 4, i % 4])
+            return tile
+
+        def load_page(i):
+            tile = three.tile([P, T2], F32, name="page", tag="page")
+            nc.sync.dma_start(tile[:], page_rows[i // 4, i % 4])
+            return tile
+
+        raw00 = load_w1(0, 0)
+        for q in range(4):
+            nc.sync.dma_start(
+                tab_sc[32 * q : 32 * q + 8, :].bitcast(I32),
+                tab_scales[:, 4 * q : 4 * q + 4, :].bitcast(I32),
+            )
+        idx = load_list(offs, "idx")
+        idx2 = load_list(offs2, "idx2")
+        raw10 = load_w1(1, 0)
+        for q in range(4):
+            nc.sync.dma_start(
+                tab2_sc[32 * q : 32 * q + 4, :, :].bitcast(I32),
+                tab2_scales[:, 4 * q : 4 * q + 4, :].bitcast(I32).rearrange("a r n -> r a n"),
+            )
+        tab_w = []
+        for a in range(2):
+            tile = keep.tile([P, T], U32, name=f"tab_w{a}", tag=f"big{a}", align_bytes=64)
+            nc.sync.dma_start(
+                tile[:].bitcast(I32), tab_words[a].rearrange("p t i -> p (t i)").bitcast(I32)
+            )
+            tab_w.append(tile)
+        chains = {0: load_chain(0)}
+        wgs_first = keep.tile([P, S], F32, name="wgs_first")
+        for q in range(4):
+            nc.sync.dma_start(wgs_first[32 * q : 32 * q + 32, :], wgs_rows[:, 0, :])
+        idx3 = load_list(offs3, "idx3")
+        pages = {0: load_page(0)}
+        idx4 = load_list(offs4, "idx4")
+        gains = keep.tile([P, 2, 4], F32, name="gains")
+        nc.sync.dma_start(gains[:], gain.rearrange("(a p t) -> p a t", a=2, t=4))
+        chains[1] = load_chain(1)
+        chains[2] = load_chain(2)
+        wgs_rest = keep.tile([P, 3, S], F32, name="wgs_rest")
+        for q in range(4):
+            nc.sync.dma_start(wgs_rest[32 * q : 32 * q + 32, :, :], wgs_rows[:, 1:4, :])
+        pages[1] = load_page(1)
+
+        codes0 = keep.tile([P, 2, BANK], U32, name="codes0", align_bytes=64)
+        quantise_w1(0, 0, raw00, codes0[:, 0, :])
+        v_sc = keep.tile([P, S], U8, name="v_sc", align_bytes=64)
+        nc.vector.tensor_copy(v_sc[:], tab_sc[:].indirect(idx[:]))
+        quantise_w1(1, 0, raw10, codes0[:, 1, :])
+        v2_sc = keep.tile([P, 2, S2], U8, name="v2_sc", align_bytes=64)
+        for a in range(2):
+            nc.vector.tensor_copy(v2_sc[:, a, :], tab2_sc[:, a, :].indirect(idx2[:]))
+        v = [keep.tile([P, S], U32, name=f"v{a}", align_bytes=64) for a in range(2)]
+        nc.vector.tensor_copy(v[0][:], tab_w[0][:].indirect(idx[:]))
+        for hh in range(2):
+            nc.vector.tensor_copy(
+                v[1][:, BANK * hh : BANK * (hh + 1)],
+                tab_w[1][:].indirect(idx[:, 32 * hh : 32 * (hh + 1)]),
+            )
+
+        def product(i, hh):
+            b, t = i // 4, i % 4
+            cols = slice(BANK * hh, BANK * (hh + 1))
+            acc = bank(hh)
+            for a in range(2):
+                nc.tensor.matmul_mx(
+                    acc[:],
+                    lhsT=w_codes[a, b][:, P * t : P * (t + 1)].bitcast(FP8X4),
+                    lhsT_scale=w_scales[a, b][:, P * t : P * (t + 1)],
+                    rhs=v[a][:, cols].bitcast(FP8X4),
+                    rhs_scale=v_sc[4 * a : P, cols],
+                    start=(a == 0),
+                    stop=(a == 1),
+                )
+            return acc
+
+        def make_h(i):
+            h = keep.tile([P, S], F32, name=f"h{i}", tag="h" + "ABCDABDE"[i], align_bytes=64)
+            for hh in range(2):
+                cols = slice(BANK * hh, BANK * (hh + 1))
+                acc = product(i, hh)
+                if i == 0:
+                    nc.vector.tensor_tensor(h[:, cols], acc[:], chains[i][:, cols], ADD)
+                    continue
+                plain = two.tile([P, BANK], F32, name="plain", tag="plain")
+                nc.scalar.copy(plain[:], acc[:])
+                turned = bank(2 + hh)
+                for n, src in enumerate((chains[i][:, cols], plain[:])):
+                    for c in range(4):
+                        blk = slice(P * c, P * (c + 1))
+                        nc.tensor.matmul(
+                            turned[:, blk], lhsT=src[:, blk], rhs=ident[:], is_transpose=True,
+                            start=(n == 0 and c == 0), stop=(n == 1 and c == 3),
+                        )
+                summed = keep.tile([P, BANK], F32, name="summed", tag=f"summed{hh}{i % 2 * hh}")
+                nc.scalar.copy(summed[:], turned[:])
+                back = bank(4 + hh)
+                for c in range(4):
+                    blk = slice(P * c, P * (c + 1))
+                    nc.tensor.transpose(back[:, blk], summed[:, blk], ident[:])
+                nc.scalar.copy(h[:, cols], back[:])
+            return h
+
+        woven = [keep.tile([P, NP, 4], BF16, name=f"woven{a}", align_bytes=64) for a in range(2)]
+
+        def through_page(i, h):
+            b, t = i // 4, i % 4
+            weights = wgs_first[:] if t == 0 else wgs_rest[:, t - 1, :]
+            page = pages[i]
+            if i == 0:
+                for hh in range(2):
+                    cols = slice(BANK * hh, BANK * (hh + 1))
+                    nc.vector.tensor_tensor(
+                        page[:].indirect(idx3[:, 32 * hh : 32 * (hh + 1)]), h[:, cols], weights[:, cols], MULT
+                    )
+            else:
+                nc.vector.tensor_tensor(page[:].indirect(idx3[:]), h[:], weights, MULT)
+            picked = keep.tile([P, NP], F32, name="picked", tag=f"summed1{(i + 1) % 2}")
+            pieces = 2 if i == 7 else 1
+            width = NP // pieces
+            for n in range(pieces):
+                cols = slice(width * n, width * (n + 1))
+                nc.vector.tensor_copy(
+                    picked[:, cols], page[:].indirect(idx4[:, width // 16 * n : width // 16 * (n + 1)])
+                )
+                nc.scalar.activation(woven[b][:, cols, t], picked[:, cols], COPY, scale=gains[:, b, t : t + 1])
+
+        hs = {0: make_h(0), 1: make_h(1)}
+        through_page(0, hs[0])
+        hs[2] = make_h(2)
+        chains[3] = load_chain(3)
+        raw01 = load_w1(0, 1)
+        pages[2] = load_page(2)
+        raw11 = load_w1(1, 1)
+        chains[4] = load_chain(4)
+        through_page(1, hs[1])
+        hs[3] = make_h(3)
+        pages[3] = load_page(3)
+        chains[5] = load_chain(5)
+        tab2_w = []
+        for a in range(2):
+            tile = keep.tile([P, T3], U32, name=f"tab2_w{a}", align_bytes=64)
+            nc.sync.dma_start(
+                tile[:].bitcast(I32), tab2_words[a].rearrange("p t i -> p (t i)").bitcast(I32)
+            )
+            tab2_w.append(tile)
+        sk_w = keep.tile([P, 2, 2 * NP], U8, name="sk_w", align_bytes=64)
+        nc.sync.dma_start(sk_w[:].bitcast(I32), sk_words.bitcast(I32).rearrange("a p n -> p a n"))
+        for q in range(4):
+            nc.sync.dma_start(
+                sk_sc[32 * q : 32 * q + 4, :, :].bitcast(I32),
+                sk_scales[:, 4 * q : 4 * q + 4, :].bitcast(I32).rearrange("a r n -> r a n"),
+            )
+        through_page(2, hs[2])
+        codes1 = keep.tile([P, 2, BANK], U32, name="codes1", tag="hC", align_bytes=64)
+        quantise_w1(0, 1, raw01, codes1[:, 0, :])
+        quantise_w1(1, 1, raw11, codes1[:, 1, :])
+        hs[4] = make_h(4)
+        pages[4] = load_page(4)
+        chains[6] = load_chain(6)
+        through_page(3, hs[3])
+        hs[5] = make_h(5)
+        pages[5] = load_page(5)
+        chains[7] = load_chain(7)
+        periods = keep.tile([P, 8, NP], F32, name="periods", tag="big0", align_bytes=64)
+        nc.sync.dma_start(periods[:], period.rearrange("(m p) j -> p m j", p=P))
+
+        v2 = [keep.tile([P, S2], U32, name=f"v2{a}", align_bytes=64) for a in range(2)]
+        for a in range(2):
+            nc.vector.tensor_copy(v2[a][:], tab2_w[a][:].indirect(idx2[:]))
+
+        through_page(4, hs[4])
+        hs[6] = make_h(6)
+        pages[6] = load_page(6)
+
+        sketch = keep.tile([P, 8, NP], F32, name="sketch", tag="big1", align_bytes=64)
+        for m in range(8):
+            rows = slice(P * m, P * (m + 1))
+            acc = bank(6 + m % 2)
+            for a in range(2):
+                nc.tensor.matmul_mx(
+                    acc[:],
+                    lhsT=v2[a][:, rows].bitcast(FP8X4),
+                    lhsT_scale=v2_sc[:, a, rows],
+                    rhs=sk_w[:, a, :].bitcast(FP4X4),
+                    rhs_scale=sk_sc[:, a, :],
+                    start=(a == 0),
+                    stop=(a == 1),
+                )
+            nc.scalar.copy(sketch[:, m, :], acc[:])
+
+        x_codes = [
+            keep.tile([P, NP], U32, name="x_codes0", tag="hA", align_bytes=64),
+            keep.tile([P, NP], U32, name="x_codes1", align_bytes=64),
+        ]
+        x_scales = [keep.tile([P, NP], U8, name=f"x_scales{a}", align_bytes=64) for a in range(2)]
+        nc.vector.quantize_mx(
+            x_codes[0][:].bitcast(FP8X4), x_scales[0][:], woven[0][:].rearrange("p j t -> p (j t)")
+        )
+
+        through_page(5, hs[5])
+        hs[7] = make_h(7)
+        pages[7] = load_page(7)
+        through_page(6, hs[6])
+
+        half = NP // 2
+        scores = {}
+
+        def score_pass(hh, mp, a):
+            cols = slice(half * hh, half * (hh + 1))
+            for n in range(2):
+                rows = slice(P * (2 * mp + n), P * (2 * mp + n + 1))
+                nc.tensor.matmul_mx(
+                    scores[hh, mp][:, half * n : half * (n + 1)],
+                    lhsT=v2[a][:, rows].bitcast(FP8X4),
+                    lhsT_scale=v2_sc[:, a, rows],
+                    rhs=x_codes[a][:, cols].bitcast(FP8X4),
+                    rhs_scale=x_scales[a][:, cols],
+                    start=(a == 0 and n == 0),
+                    stop=(a == 1 and n == 1),
+                )
+
+        for hh in range(2):
+            for mp in range(4):
+                scores[hh, mp] = bank(4 * hh + mp)
+                score_pass(hh, mp, 0)
+
+        through_page(7, hs[7])
+
+        out_rows = out.rearrange("(m p) j -> p m j", p=P)
+        for hh in range(2):
+            cols = slice(half * hh, half * (hh + 1))
+            nc.vector.quantize_mx(
+                x_codes[1][:, cols].bitcast(FP8X4),
+                x_scales[1][:, cols],
+                woven[1][:, cols, :].rearrange("p j t -> p (j t)"),
+            )
+            for mp in range(4):
+                score_pass(hh, mp, 1)
+        for hh in range(2):
+            cols = slice(half * hh, half * (hh + 1))
+            for mp in range(4):
+                pair = slice(2 * mp, 2 * mp + 2)
+                bounded = three.tile([P, 2, half], F32, name="bounded", tag="bounded")
+                nc.scalar.activation(
+                    bounded[:], scores[hh, mp][:].rearrange("p (n j) -> p n j", n=2), TANH
+                )
+                weighted = two.tile([P, 2, half], F32, name="weighted", tag="weighted")
+                nc.vector.tensor_tensor(weighted[:], bounded[:], periods[:, pair, cols], MULT)
+                result = three.tile([P, 2, half], F32, name="result", tag="result")
+                nc.vector.tensor_tensor(result[:], weighted[:], sketch[:, pair, cols], MAX)
+                nc.sync.dma_start(out_rows[:, pair, cols], result[:])

@@ -22,6 +22,7 @@ TANH = mybir.ActivationFunctionType.Tanh
 
 P = 128
 BANK = 512
+ADD_ON_VECTOR = (0, 1, 2, 4)
 
 
 def tile_list_watermark_candidate_scores_kernel(
@@ -44,93 +45,122 @@ def tile_list_watermark_candidate_scores_kernel(
             nc.sync.dma_start(tile[:], src)
             return tile
 
-        chain_rows = chain.rearrange("(a p t) j -> a t p j", a=2, t=4)
-        page_rows = page0.rearrange("(a p t) c -> a t p c", a=2, t=4)
-        wgs_rows = wgs.rearrange("(q t) j -> q t j", t=4)
+        def tile_rows(src, i):
+            if i < 4:
+                return src[P * i : P * (i + 1), :]
+            return src[512:1024, :].rearrange("(p t) c -> t p c", t=4)[i - 4]
 
-        tab_sc = keep.tile([P, T], U8, name="tab_sc", align_bytes=64)
-        nc.vector.memset(tab_sc[:].bitcast(I32), 0)
-        tab2_sc = keep.tile([P, 2, T3], U8, name="tab2_sc", align_bytes=64)
-        nc.vector.memset(tab2_sc[:].bitcast(I32), 0)
-        sk_sc = keep.tile([P, 2, NP], U8, name="sk_sc", align_bytes=64)
-        nc.gpsimd.memset(sk_sc[:].bitcast(I32), 0)
-        ident = keep.tile([P, P], F32, name="ident")
-        make_identity(nc, ident[:])
+        def scale_window(src, width, name):
+            tile = keep.tile([P, width], U8, name=name, align_bytes=64)
+            nc.vector.memset(tile[32:64, :].bitcast(I32), 0)
+            nc.vector.memset(tile[64:128, :].bitcast(I32), 0)
+            for a in range(2):
+                nc.sync.dma_start(tile[a:32:2, :].bitcast(I32), src[a].bitcast(I32))
+            return tile
 
-        w_codes = {}
-        w_scales = {}
+        def zeroed_planes(width, name):
+            tile = keep.tile([P, 2, width], U8, name=name, align_bytes=64)
+            nc.gpsimd.memset(tile[:].bitcast(I32), 0)
+            return tile
 
-        def load_w1(a, b):
-            raw = two.tile([P, 4, BANK], F32, name="w_raw", tag="w_raw")
-            rows = w1[512 * a : 512 * (a + 1), 512 * b : 512 * (b + 1)]
+        def place_scales(planes, picked_rows):
+            for q in range(4):
+                nc.sync.dma_start(
+                    planes[32 * q : 32 * q + 4, :, :].bitcast(I32),
+                    picked_rows[8 * q : 8 * q + 8, :].bitcast(I32),
+                )
+
+        def load_words(src, tile):
+            nc.sync.dma_start(tile[:].bitcast(I32), src.rearrange("p t i -> p (t i)").bitcast(I32))
+
+        def load_w1_pair(first):
+            raw = two.tile([P, 2, 4, 256], F32, name="w_raw", tag="raw", align_bytes=64)
+            for a in range(2):
+                rows = w1[512 * a : 512 * (a + 1), first : first + 256]
+                nc.sync.dma_start(raw[:, a, :, :], rows.rearrange("(p j) c -> p j c", j=4))
+            return raw
+
+        def load_w1_dealt(a):
+            raw = two.tile([P, 4, BANK], F32, name="w_raw", tag="raw", align_bytes=64)
+            rows = w1[512 * a : 512 * (a + 1), 512:1024]
             nc.sync.dma_start(raw[:], rows.rearrange("(p j) c -> p j c", j=4))
             return raw
 
-        def quantise_w1(a, b, raw, codes):
+        weights = {}
+
+        def quantise_w1_pair(raw, first_tile, tag):
+            grouped = two.tile([P, 2, 1024], BF16, name="w_grouped", tag="w_grouped", align_bytes=64)
+            for a in range(2):
+                nc.scalar.copy(
+                    grouped[:, a, :].rearrange("p (c i j) -> p c j i", i=4, j=4),
+                    raw[:, a, :, :].rearrange("p j (c i) -> p c j i", i=4),
+                )
+            codes = keep.tile([P, BANK], U32, name="w_codes", tag=tag, align_bytes=64)
+            scales = keep.tile([P, BANK], U8, name=f"w_scales{first_tile}", align_bytes=64)
+            nc.vector.quantize_mx(codes[:].bitcast(FP8X4), scales[:], grouped[:].rearrange("p a n -> p (a n)"))
+            for n in range(2):
+                for a in range(2):
+                    cols = slice(256 * a + P * n, 256 * a + P * (n + 1))
+                    weights[first_tile + n, a] = (codes[:, cols], scales[:, cols])
+
+        def quantise_w1_dealt(a, raw, codes, scales):
             grouped = two.tile([P, 4 * BANK], BF16, name="w_grouped", tag="w_grouped", align_bytes=64)
             nc.scalar.copy(
                 grouped[:].rearrange("p (t m j) -> p m t j", t=4, j=4),
                 raw[:].rearrange("p j (m t) -> p m t j", t=4),
             )
-            w_codes[a, b] = codes
-            w_scales[a, b] = keep.tile([P, BANK], U8, name=f"w_scales{a}{b}", align_bytes=64)
-            nc.vector.quantize_mx(codes.bitcast(FP8X4), w_scales[a, b][:], grouped[:])
+            nc.vector.quantize_mx(codes.bitcast(FP8X4), scales, grouped[:])
+            for t in range(4):
+                cols = slice(P * t, P * (t + 1))
+                weights[4 + t, a] = (codes[:, cols], scales[:, cols])
+
+        chains = {}
+        pages = {}
 
         def load_chain(i):
-            tile = three.tile([P, S], F32, name="chain", tag="chain")
-            nc.sync.dma_start(tile[:], chain_rows[i // 4, i % 4])
-            return tile
+            chains[i] = three.tile([P, S], F32, name="chain", tag="chain")
+            nc.sync.dma_start(chains[i][:], tile_rows(chain, i))
 
         def load_page(i):
-            tile = three.tile([P, T2], F32, name="page", tag="page")
-            nc.sync.dma_start(tile[:], page_rows[i // 4, i % 4])
-            return tile
+            pages[i] = three.tile([P, T2], F32, name="page", tag="page")
+            nc.sync.dma_start(pages[i][:], tile_rows(page0, i))
 
-        raw00 = load_w1(0, 0)
-        for q in range(4):
-            nc.sync.dma_start(
-                tab_sc[32 * q : 32 * q + 8, :].bitcast(I32),
-                tab_scales[:, 4 * q : 4 * q + 4, :].bitcast(I32),
-            )
+        v_planes = zeroed_planes(S, "v_planes")
+        ident = keep.tile([P, P], F32, name="ident")
+        make_identity(nc, ident[:])
+        v2_planes = zeroed_planes(S2, "v2_planes")
+        sk_planes = zeroed_planes(NP, "sk_planes")
+
+        tab_sc = scale_window(tab_scales, T, "tab_sc")
         idx = load_list(offs, "idx")
+        raw_first = load_w1_pair(0)
+        tab2_sc = scale_window(tab2_scales, T3, "tab2_sc")
         idx2 = load_list(offs2, "idx2")
-        raw10 = load_w1(1, 0)
-        for q in range(4):
-            nc.sync.dma_start(
-                tab2_sc[32 * q : 32 * q + 4, :, :].bitcast(I32),
-                tab2_scales[:, 4 * q : 4 * q + 4, :].bitcast(I32).rearrange("a r n -> r a n"),
-            )
-        tab_w = []
-        for a in range(2):
-            tile = keep.tile([P, T], U32, name=f"tab_w{a}", tag=f"big{a}", align_bytes=64)
-            nc.sync.dma_start(
-                tile[:].bitcast(I32), tab_words[a].rearrange("p t i -> p (t i)").bitcast(I32)
-            )
-            tab_w.append(tile)
-        chains = {0: load_chain(0)}
-        wgs_first = keep.tile([P, S], F32, name="wgs_first")
-        for q in range(4):
-            nc.sync.dma_start(wgs_first[32 * q : 32 * q + 32, :], wgs_rows[:, 0, :])
-        idx3 = load_list(offs3, "idx3")
-        pages = {0: load_page(0)}
-        idx4 = load_list(offs4, "idx4")
-        gains = keep.tile([P, 2, 4], F32, name="gains")
-        nc.sync.dma_start(gains[:], gain.rearrange("(a p t) -> p a t", a=2, t=4))
-        chains[1] = load_chain(1)
-        chains[2] = load_chain(2)
-        wgs_rest = keep.tile([P, 3, S], F32, name="wgs_rest")
-        for q in range(4):
-            nc.sync.dma_start(wgs_rest[32 * q : 32 * q + 32, :, :], wgs_rows[:, 1:4, :])
-        pages[1] = load_page(1)
+        tab_w = [keep.tile([P, T], U32, name=f"tab_w{a}", tag=f"big{a}", align_bytes=64) for a in range(2)]
+        load_words(tab_words[0], tab_w[0])
 
-        codes0 = keep.tile([P, 2, BANK], U32, name="codes0", align_bytes=64)
-        quantise_w1(0, 0, raw00, codes0[:, 0, :])
         v_sc = keep.tile([P, S], U8, name="v_sc", align_bytes=64)
         nc.vector.tensor_copy(v_sc[:], tab_sc[:].indirect(idx[:]))
-        quantise_w1(1, 0, raw10, codes0[:, 1, :])
-        v2_sc = keep.tile([P, 2, S2], U8, name="v2_sc", align_bytes=64)
-        for a in range(2):
-            nc.vector.tensor_copy(v2_sc[:, a, :], tab2_sc[:, a, :].indirect(idx2[:]))
+        place_scales(v_planes, v_sc)
+        load_words(tab_words[1], tab_w[1])
+
+        chains[0] = three.tile([P, S], F32, name="chain", tag="chain")
+        wgs_plain = keep.tile([P, S], F32, name="wgs_plain")
+        nc.sync.dma_start(chains[0][:, :BANK], tile_rows(chain, 0)[:, :BANK])
+        nc.sync.dma_start(wgs_plain[:, :BANK], wgs[:, :BANK])
+        idx3 = load_list(offs3, "idx3")
+        load_page(0)
+        nc.sync.dma_start(chains[0][:, BANK:], tile_rows(chain, 0)[:, BANK:])
+        nc.sync.dma_start(wgs_plain[:, BANK:], wgs[:, BANK:])
+        idx4 = load_list(offs4, "idx4")
+        load_chain(1)
+        raw_second = load_w1_pair(256)
+        load_page(1)
+        load_chain(2)
+
+        v2_sc = keep.tile([P, S2], U8, name="v2_sc", align_bytes=64)
+        nc.vector.tensor_copy(v2_sc[:], tab2_sc[:].indirect(idx2[:]))
+        quantise_w1_pair(raw_first, 0, "codes_first")
         v = [keep.tile([P, S], U32, name=f"v{a}", align_bytes=64) for a in range(2)]
         nc.vector.tensor_copy(v[0][:], tab_w[0][:].indirect(idx[:]))
         for hh in range(2):
@@ -139,31 +169,29 @@ def tile_list_watermark_candidate_scores_kernel(
                 tab_w[1][:].indirect(idx[:, 32 * hh : 32 * (hh + 1)]),
             )
 
-        def product(i, hh):
-            b, t = i // 4, i % 4
-            cols = slice(BANK * hh, BANK * (hh + 1))
-            acc = bank(hh)
-            for a in range(2):
-                nc.tensor.matmul_mx(
-                    acc[:],
-                    lhsT=w_codes[a, b][:, P * t : P * (t + 1)].bitcast(FP8X4),
-                    lhsT_scale=w_scales[a, b][:, P * t : P * (t + 1)],
-                    rhs=v[a][:, cols].bitcast(FP8X4),
-                    rhs_scale=v_sc[4 * a : P, cols],
-                    start=(a == 0),
-                    stop=(a == 1),
-                )
-            return acc
+        hs = {}
 
         def make_h(i):
-            h = keep.tile([P, S], F32, name=f"h{i}", tag="h" + "ABCDABDE"[i], align_bytes=64)
+            h = keep.tile([P, S], F32, name=f"h{i}", tag="h" + "ABFCBDEC"[i], align_bytes=64)
+            hs[i] = h
             for hh in range(2):
                 cols = slice(BANK * hh, BANK * (hh + 1))
-                acc = product(i, hh)
-                if i == 0:
+                acc = bank(hh if i not in ADD_ON_VECTOR else 6 + hh)
+                for a in range(2):
+                    codes, scales = weights[i, a]
+                    nc.tensor.matmul_mx(
+                        acc[:],
+                        lhsT=codes.bitcast(FP8X4),
+                        lhsT_scale=scales,
+                        rhs=v[a][:, cols].bitcast(FP8X4),
+                        rhs_scale=v_planes[:, a, cols],
+                        start=(a == 0),
+                        stop=(a == 1),
+                    )
+                if i in ADD_ON_VECTOR:
                     nc.vector.tensor_tensor(h[:, cols], acc[:], chains[i][:, cols], ADD)
                     continue
-                plain = two.tile([P, BANK], F32, name="plain", tag="plain")
+                plain = keep.tile([P, BANK], F32, name="plain", tag=f"plain{hh}", align_bytes=64)
                 nc.scalar.copy(plain[:], acc[:])
                 turned = bank(2 + hh)
                 for n, src in enumerate((chains[i][:, cols], plain[:])):
@@ -173,116 +201,145 @@ def tile_list_watermark_candidate_scores_kernel(
                             turned[:, blk], lhsT=src[:, blk], rhs=ident[:], is_transpose=True,
                             start=(n == 0 and c == 0), stop=(n == 1 and c == 3),
                         )
-                summed = keep.tile([P, BANK], F32, name="summed", tag=f"summed{hh}{i % 2 * hh}")
+                summed = keep.tile([P, BANK], F32, name="summed", tag=f"summed{hh}", align_bytes=64)
                 nc.scalar.copy(summed[:], turned[:])
                 back = bank(4 + hh)
                 for c in range(4):
                     blk = slice(P * c, P * (c + 1))
                     nc.tensor.transpose(back[:, blk], summed[:, blk], ident[:])
                 nc.scalar.copy(h[:, cols], back[:])
-            return h
 
-        woven = [keep.tile([P, NP, 4], BF16, name=f"woven{a}", align_bytes=64) for a in range(2)]
+        picked = {}
 
-        def through_page(i, h):
-            b, t = i // 4, i % 4
-            weights = wgs_first[:] if t == 0 else wgs_rest[:, t - 1, :]
-            page = pages[i]
-            if i == 0:
-                for hh in range(2):
-                    cols = slice(BANK * hh, BANK * (hh + 1))
-                    nc.vector.tensor_tensor(
-                        page[:].indirect(idx3[:, 32 * hh : 32 * (hh + 1)]), h[:, cols], weights[:, cols], MULT
-                    )
-            else:
-                nc.vector.tensor_tensor(page[:].indirect(idx3[:]), h[:], weights, MULT)
-            picked = keep.tile([P, NP], F32, name="picked", tag=f"summed1{(i + 1) % 2}")
-            pieces = 2 if i == 7 else 1
-            width = NP // pieces
+        def scatter(i, pieces=1):
+            factors = wgs_plain[:] if i < 4 else wgs_dealt[:, i - 4, :]
+            width = S // pieces
             for n in range(pieces):
                 cols = slice(width * n, width * (n + 1))
-                nc.vector.tensor_copy(
-                    picked[:, cols], page[:].indirect(idx4[:, width // 16 * n : width // 16 * (n + 1)])
+                nc.vector.tensor_tensor(
+                    pages[i][:].indirect(idx3[:, width // 16 * n : width // 16 * (n + 1)]),
+                    hs[i][:, cols], factors[:, cols], MULT,
                 )
-                nc.scalar.activation(woven[b][:, cols, t], picked[:, cols], COPY, scale=gains[:, b, t : t + 1])
 
-        hs = {0: make_h(0), 1: make_h(1)}
-        through_page(0, hs[0])
-        hs[2] = make_h(2)
-        chains[3] = load_chain(3)
-        raw01 = load_w1(0, 1)
-        pages[2] = load_page(2)
-        raw11 = load_w1(1, 1)
-        chains[4] = load_chain(4)
-        through_page(1, hs[1])
-        hs[3] = make_h(3)
-        pages[3] = load_page(3)
-        chains[5] = load_chain(5)
-        tab2_w = []
+        def fetch(i, pieces=1):
+            picked[i] = keep.tile([P, NP], F32, name="picked", tag=f"picked{i % 4}")
+            width = NP // pieces
+            for n in range(pieces):
+                nc.vector.tensor_copy(
+                    picked[i][:, width * n : width * (n + 1)],
+                    pages[i][:].indirect(idx4[:, width // 16 * n : width // 16 * (n + 1)]),
+                )
+
+        regrouped = keep.tile([P, 4, NP], F32, name="regrouped")
+
+        def regroup(i):
+            nc.sync.dma_start(regrouped[32 * i : 32 * (i + 1), :, :], picked[i][:])
+
+        make_h(0)
+        scatter(0, pieces=2)
+        fetch(0)
+        make_h(1)
+        quantise_w1_pair(raw_second, 2, "hA")
+        raw_dealt = [load_w1_dealt(a) for a in range(2)]
+        load_chain(3)
+        load_page(2)
+        regroup(0)
+        load_page(3)
+        scatter(1)
+        fetch(1)
+        make_h(2)
+        make_h(3)
+        load_chain(4)
+        load_chain(5)
+        wgs_dealt = keep.tile([P, 4, S], F32, name="wgs_dealt")
+        for q in range(4):
+            nc.sync.dma_start(wgs_dealt[32 * q : 32 * q + 32, :, :], wgs.rearrange("(q t) j -> q t j", t=4))
+        regroup(1)
+        load_page(4)
+        scatter(2)
+        fetch(2)
+        codes_dealt = keep.tile([P, 2, BANK], U32, name="codes_dealt", tag="hF", align_bytes=64)
+        scales_dealt = keep.tile([P, 2, BANK], U8, name="scales_dealt", align_bytes=64)
         for a in range(2):
-            tile = keep.tile([P, T3], U32, name=f"tab2_w{a}", align_bytes=64)
-            nc.sync.dma_start(
-                tile[:].bitcast(I32), tab2_words[a].rearrange("p t i -> p (t i)").bitcast(I32)
-            )
-            tab2_w.append(tile)
+            quantise_w1_dealt(a, raw_dealt[a], codes_dealt[:, a, :], scales_dealt[:, a, :])
+        load_chain(6)
+        scatter(3)
+        fetch(3)
+        make_h(4)
+        make_h(5)
+
+        tab2_w = [two.tile([P, T3], U32, name="tab2_w", tag="raw", align_bytes=64) for a in range(2)]
+        for a in range(2):
+            load_words(tab2_words[a], tab2_w[a])
+        place_scales(v2_planes, v2_sc)
+        load_chain(7)
+        regroup(2)
+        load_page(5)
         sk_w = keep.tile([P, 2, 2 * NP], U8, name="sk_w", align_bytes=64)
         nc.sync.dma_start(sk_w[:].bitcast(I32), sk_words.bitcast(I32).rearrange("a p n -> p a n"))
         for q in range(4):
             nc.sync.dma_start(
-                sk_sc[32 * q : 32 * q + 4, :, :].bitcast(I32),
+                sk_planes[32 * q : 32 * q + 4, :, :].bitcast(I32),
                 sk_scales[:, 4 * q : 4 * q + 4, :].bitcast(I32).rearrange("a r n -> r a n"),
             )
-        through_page(2, hs[2])
-        codes1 = keep.tile([P, 2, BANK], U32, name="codes1", tag="hC", align_bytes=64)
-        quantise_w1(0, 1, raw01, codes1[:, 0, :])
-        quantise_w1(1, 1, raw11, codes1[:, 1, :])
-        hs[4] = make_h(4)
-        pages[4] = load_page(4)
-        chains[6] = load_chain(6)
-        through_page(3, hs[3])
-        hs[5] = make_h(5)
-        pages[5] = load_page(5)
-        chains[7] = load_chain(7)
+        gains = keep.tile([P, 2, 4], F32, name="gains")
+        nc.sync.dma_start(gains[:], gain.rearrange("(a p t) -> p a t", a=2, t=4))
+        regroup(3)
+        load_page(6)
         periods = keep.tile([P, 8, NP], F32, name="periods", tag="big0", align_bytes=64)
         nc.sync.dma_start(periods[:], period.rearrange("(m p) j -> p m j", p=P))
 
+        scatter(4)
+        fetch(4)
+        load_page(7)
         v2 = [keep.tile([P, S2], U32, name=f"v2{a}", align_bytes=64) for a in range(2)]
         for a in range(2):
             nc.vector.tensor_copy(v2[a][:], tab2_w[a][:].indirect(idx2[:]))
+        make_h(6)
+        make_h(7)
 
-        through_page(4, hs[4])
-        hs[6] = make_h(6)
-        pages[6] = load_page(6)
+        woven = [
+            keep.tile([P, NP, 4], BF16, name="woven0", tag="summed1", align_bytes=64),
+            keep.tile([P, NP, 4], BF16, name="woven1", tag="plain1", align_bytes=64),
+        ]
+
+        def weave(a, t, src, cols):
+            nc.scalar.activation(woven[a][:, cols, t], src, COPY, scale=gains[:, a, t : t + 1])
+
+        every = slice(0, NP)
+        for t in range(4):
+            weave(0, t, regrouped[:, t, :], every)
 
         sketch = keep.tile([P, 8, NP], F32, name="sketch", tag="big1", align_bytes=64)
         for m in range(8):
             rows = slice(P * m, P * (m + 1))
-            acc = bank(6 + m % 2)
+            acc = bank(m % 4)
             for a in range(2):
                 nc.tensor.matmul_mx(
                     acc[:],
                     lhsT=v2[a][:, rows].bitcast(FP8X4),
-                    lhsT_scale=v2_sc[:, a, rows],
+                    lhsT_scale=v2_planes[:, a, rows],
                     rhs=sk_w[:, a, :].bitcast(FP4X4),
-                    rhs_scale=sk_sc[:, a, :],
+                    rhs_scale=sk_planes[:, a, :],
                     start=(a == 0),
                     stop=(a == 1),
                 )
             nc.scalar.copy(sketch[:, m, :], acc[:])
 
+        weave(1, 0, picked[4][:], every)
+        for i in (5, 6):
+            scatter(i)
+            fetch(i)
+            weave(1, i - 4, picked[i][:], every)
+
         x_codes = [
-            keep.tile([P, NP], U32, name="x_codes0", tag="hA", align_bytes=64),
+            keep.tile([P, NP], U32, name="x_codes0", tag="hE", align_bytes=64),
             keep.tile([P, NP], U32, name="x_codes1", align_bytes=64),
         ]
         x_scales = [keep.tile([P, NP], U8, name=f"x_scales{a}", align_bytes=64) for a in range(2)]
         nc.vector.quantize_mx(
             x_codes[0][:].bitcast(FP8X4), x_scales[0][:], woven[0][:].rearrange("p j t -> p (j t)")
         )
-
-        through_page(5, hs[5])
-        hs[7] = make_h(7)
-        pages[7] = load_page(7)
-        through_page(6, hs[6])
 
         half = NP // 2
         scores = {}
@@ -294,7 +351,7 @@ def tile_list_watermark_candidate_scores_kernel(
                 nc.tensor.matmul_mx(
                     scores[hh, mp][:, half * n : half * (n + 1)],
                     lhsT=v2[a][:, rows].bitcast(FP8X4),
-                    lhsT_scale=v2_sc[:, a, rows],
+                    lhsT_scale=v2_planes[:, a, rows],
                     rhs=x_codes[a][:, cols].bitcast(FP8X4),
                     rhs_scale=x_scales[a][:, cols],
                     start=(a == 0 and n == 0),
@@ -306,11 +363,13 @@ def tile_list_watermark_candidate_scores_kernel(
                 scores[hh, mp] = bank(4 * hh + mp)
                 score_pass(hh, mp, 0)
 
-        through_page(7, hs[7])
+        scatter(7)
+        fetch(7, pieces=2)
 
         out_rows = out.rearrange("(m p) j -> p m j", p=P)
         for hh in range(2):
             cols = slice(half * hh, half * (hh + 1))
+            weave(1, 3, picked[7][:, cols], cols)
             nc.vector.quantize_mx(
                 x_codes[1][:, cols].bitcast(FP8X4),
                 x_scales[1][:, cols],

@@ -22,7 +22,7 @@ TANH = mybir.ActivationFunctionType.Tanh
 
 P = 128
 BANK = 512
-ADD_ON_VECTOR = (0, 1, 2, 4)
+ADD_ON_VECTOR = (0, 1, 2)
 
 
 def tile_list_watermark_candidate_scores_kernel(
@@ -35,6 +35,7 @@ def tile_list_watermark_candidate_scores_kernel(
         keep = ctx.enter_context(tc.tile_pool(name="keep", bufs=1))
         two = ctx.enter_context(tc.tile_pool(name="two", bufs=2))
         three = ctx.enter_context(tc.tile_pool(name="three", bufs=3))
+        four = ctx.enter_context(tc.tile_pool(name="four", bufs=4))
         psum = ctx.enter_context(tc.psum_pool(name="psum", bufs=1))
 
         def bank(b):
@@ -122,7 +123,7 @@ def tile_list_watermark_candidate_scores_kernel(
             nc.sync.dma_start(chains[i][:], tile_rows(chain, i))
 
         def load_page(i):
-            pages[i] = three.tile([P, T2], F32, name="page", tag="page")
+            pages[i] = four.tile([P, T2], F32, name="page", tag="page")
             nc.sync.dma_start(pages[i][:], tile_rows(page0, i))
 
         v_planes = zeroed_planes(S, "v_planes")
@@ -152,8 +153,8 @@ def tile_list_watermark_candidate_scores_kernel(
         load_page(0)
         nc.sync.dma_start(chains[0][:, BANK:], tile_rows(chain, 0)[:, BANK:])
         nc.sync.dma_start(wgs_plain[:, BANK:], wgs[:, BANK:])
-        idx4 = load_list(offs4, "idx4")
         load_chain(1)
+        idx4 = load_list(offs4, "idx4")
         raw_second = load_w1_pair(256)
         load_page(1)
         load_chain(2)
@@ -230,51 +231,57 @@ def tile_list_watermark_candidate_scores_kernel(
                     pages[i][:].indirect(idx4[:, width // 16 * n : width // 16 * (n + 1)]),
                 )
 
-        regrouped = keep.tile([P, 4, NP], F32, name="regrouped")
+        regrouped = keep.tile([P, 4, NP], F32, name="regrouped", tag="regrouped")
 
         def regroup(i):
             nc.sync.dma_start(regrouped[32 * i : 32 * (i + 1), :, :], picked[i][:])
 
+        wgs_dealt = keep.tile([P, 4, S], F32, name="wgs_dealt")
+
+        def load_wgs_dealt(t):
+            rows = wgs.rearrange("(q t) j -> t q j", t=4)[t]
+            for q in range(4):
+                nc.sync.dma_start(wgs_dealt[32 * q : 32 * q + 32, t, :], rows)
+
         make_h(0)
         scatter(0, pieces=2)
-        fetch(0)
         make_h(1)
+        fetch(0)
         quantise_w1_pair(raw_second, 2, "hA")
-        raw_dealt = [load_w1_dealt(a) for a in range(2)]
+        raw_dealt = [load_w1_dealt(0)]
         load_chain(3)
         load_page(2)
-        regroup(0)
-        load_page(3)
-        scatter(1)
-        fetch(1)
-        make_h(2)
-        make_h(3)
+        raw_dealt.append(load_w1_dealt(1))
         load_chain(4)
-        load_chain(5)
-        wgs_dealt = keep.tile([P, 4, S], F32, name="wgs_dealt")
-        for q in range(4):
-            nc.sync.dma_start(wgs_dealt[32 * q : 32 * q + 32, :, :], wgs.rearrange("(q t) j -> q t j", t=4))
-        regroup(1)
+        load_page(3)
+        load_wgs_dealt(0)
         load_page(4)
+        scatter(1)
+        make_h(2)
+        fetch(1)
+        make_h(3)
+        load_chain(5)
+        load_chain(6)
+        regroup(0)
+        regroup(1)
+        load_wgs_dealt(1)
         scatter(2)
         fetch(2)
         codes_dealt = keep.tile([P, 2, BANK], U32, name="codes_dealt", tag="hF", align_bytes=64)
         scales_dealt = keep.tile([P, 2, BANK], U8, name="scales_dealt", align_bytes=64)
         for a in range(2):
             quantise_w1_dealt(a, raw_dealt[a], codes_dealt[:, a, :], scales_dealt[:, a, :])
-        load_chain(6)
-        scatter(3)
-        fetch(3)
         make_h(4)
-        make_h(5)
-
+        load_chain(7)
         tab2_w = [two.tile([P, T3], U32, name="tab2_w", tag="raw", align_bytes=64) for a in range(2)]
         for a in range(2):
             load_words(tab2_words[a], tab2_w[a])
         place_scales(v2_planes, v2_sc)
-        load_chain(7)
-        regroup(2)
         load_page(5)
+        scatter(3)
+        fetch(3)
+        regroup(2)
+        regroup(3)
         sk_w = keep.tile([P, 2, 2 * NP], U8, name="sk_w", align_bytes=64)
         nc.sync.dma_start(sk_w[:].bitcast(I32), sk_words.bitcast(I32).rearrange("a p n -> p a n"))
         for q in range(4):
@@ -284,14 +291,15 @@ def tile_list_watermark_candidate_scores_kernel(
             )
         gains = keep.tile([P, 2, 4], F32, name="gains")
         nc.sync.dma_start(gains[:], gain.rearrange("(a p t) -> p a t", a=2, t=4))
-        regroup(3)
+        load_wgs_dealt(2)
         load_page(6)
+        load_wgs_dealt(3)
+        load_page(7)
         periods = keep.tile([P, 8, NP], F32, name="periods", tag="big0", align_bytes=64)
         nc.sync.dma_start(periods[:], period.rearrange("(m p) j -> p m j", p=P))
-
+        make_h(5)
         scatter(4)
         fetch(4)
-        load_page(7)
         v2 = [keep.tile([P, S2], U32, name=f"v2{a}", align_bytes=64) for a in range(2)]
         for a in range(2):
             nc.vector.tensor_copy(v2[a][:], tab2_w[a][:].indirect(idx2[:]))
@@ -377,16 +385,26 @@ def tile_list_watermark_candidate_scores_kernel(
             )
             for mp in range(4):
                 score_pass(hh, mp, 1)
-        for hh in range(2):
+        chunks = [(hh, mp) for hh in range(2) for mp in range(4)]
+        weighted = {}
+        results = [four.tile([P, 8, half], F32, name="results", tag="page") for hh in range(2)]
+
+        def weigh(hh, mp):
             cols = slice(half * hh, half * (hh + 1))
-            for mp in range(4):
-                pair = slice(2 * mp, 2 * mp + 2)
-                bounded = three.tile([P, 2, half], F32, name="bounded", tag="bounded")
-                nc.scalar.activation(
-                    bounded[:], scores[hh, mp][:].rearrange("p (n j) -> p n j", n=2), TANH
-                )
-                weighted = two.tile([P, 2, half], F32, name="weighted", tag="weighted")
-                nc.vector.tensor_tensor(weighted[:], bounded[:], periods[:, pair, cols], MULT)
-                result = three.tile([P, 2, half], F32, name="result", tag="result")
-                nc.vector.tensor_tensor(result[:], weighted[:], sketch[:, pair, cols], MAX)
-                nc.sync.dma_start(out_rows[:, pair, cols], result[:])
+            bounded = three.tile([P, 2, half], F32, name="bounded", tag="bounded")
+            nc.scalar.activation(bounded[:], scores[hh, mp][:].rearrange("p (n j) -> p n j", n=2), TANH)
+            weighted[hh, mp] = three.tile([P, 2, half], F32, name="weighted", tag="weighted")
+            nc.vector.tensor_tensor(weighted[hh, mp][:], bounded[:], periods[:, 2 * mp : 2 * mp + 2, cols], MULT)
+
+        def finish(hh, mp):
+            cols = slice(half * hh, half * (hh + 1))
+            pair = slice(2 * mp, 2 * mp + 2)
+            result = results[hh][:, pair, :]
+            nc.vector.tensor_tensor(result, weighted[hh, mp][:], sketch[:, pair, cols], MAX)
+            nc.sync.dma_start(out_rows[:, pair, cols], result)
+
+        weigh(*chunks[0])
+        for n in range(1, len(chunks)):
+            weigh(*chunks[n])
+            finish(*chunks[n - 1])
+        finish(*chunks[-1])

from contextlib import ExitStack

import concourse.mybir as mybir
from concourse.masks import make_identity

K, H, T, S, T2, NP, T3, S2 = 1024, 1024, 4096, 1024, 2048, 512, 2048, 1024
FLOPS = 2 * K * H * S + 2 * 2 * H * S2 * NP

F32 = mybir.dt.float32
BF16 = mybir.dt.bfloat16
I32 = mybir.dt.int32
U32 = mybir.dt.uint32
U16 = mybir.dt.uint16
U8 = mybir.dt.uint8
FP8X4 = mybir.dt.float8_e4m3fn_x4
FP4X4 = mybir.dt.float4_e2m1fn_x4
MULT = mybir.AluOpType.mult
ADD = mybir.AluOpType.add
MAX = mybir.AluOpType.max
COPY = mybir.ActivationFunctionType.Copy
TANH = mybir.ActivationFunctionType.Tanh

P = 128
BANK = 512
ADD_ON_VECTOR = (0, 1, 2)


def tile_list_watermark_candidate_scores_kernel(
    tc, tab_words, tab_scales, offs, w1, chain, page0, wgs, offs3, offs4, gain,
    tab2_words, tab2_scales, offs2, sk_words, sk_scales, period, out,
):
    nc = tc.nc
    with ExitStack() as ctx:
        lists = ctx.enter_context(tc.tile_pool(name="lists", bufs=1))
        keep = ctx.enter_context(tc.tile_pool(name="keep", bufs=1))
        two = ctx.enter_context(tc.tile_pool(name="two", bufs=2))
        three = ctx.enter_context(tc.tile_pool(name="three", bufs=3))
        four = ctx.enter_context(tc.tile_pool(name="four", bufs=4))
        psum = ctx.enter_context(tc.psum_pool(name="psum", bufs=1))

        def bank(b):
            return psum.tile([P, BANK], F32, name=f"bank{b}", tag=f"bank{b}")

        def load_list(src, name):
            tile = lists.tile(list(src.shape), U16, name=name)
            nc.sync.dma_start(tile[:], src)
            return tile

        def tile_rows(src, i):
            if i < 4:
                return src[P * i : P * (i + 1), :]
            return src[512:1024, :].rearrange("(p t) c -> t p c", t=4)[i - 4]

        def scale_window(src, width, name):
            tile = keep.tile([P, width], U8, name=name, align_bytes=64)
            nc.vector.memset(tile[32:64, :].bitcast(I32), 0)
            nc.vector.memset(tile[64:128, :].bitcast(I32), 0)
            for a in range(2):
                nc.sync.dma_start(tile[a:32:2, :].bitcast(I32), src[a].bitcast(I32))
            return tile

        def zeroed_planes(width, name):
            tile = keep.tile([P, 2, width], U8, name=name, align_bytes=64)
            nc.gpsimd.memset(tile[:].bitcast(I32), 0)
            return tile

        def place_scales(planes, picked_rows):
            for q in range(4):
                nc.sync.dma_start(
                    planes[32 * q : 32 * q + 4, :, :].bitcast(I32),
                    picked_rows[8 * q : 8 * q + 8, :].bitcast(I32),
                )

        def load_words(src, tile):
            nc.sync.dma_start(tile[:].bitcast(I32), src.rearrange("p t i -> p (t i)").bitcast(I32))

        def load_w1_pair(first):
            raw = two.tile([P, 2, 4, 256], F32, name="w_raw", tag="raw", align_bytes=64)
            for a in range(2):
                rows = w1[512 * a : 512 * (a + 1), first : first + 256]
                nc.sync.dma_start(raw[:, a, :, :], rows.rearrange("(p j) c -> p j c", j=4))
            return raw

        def load_w1_dealt(a):
            raw = two.tile([P, 4, BANK], F32, name="w_raw", tag="raw", align_bytes=64)
            rows = w1[512 * a : 512 * (a + 1), 512:1024]
            nc.sync.dma_start(raw[:], rows.rearrange("(p j) c -> p j c", j=4))
            return raw

        weights = {}

        def quantise_w1_pair(raw, first_tile, tag):
            grouped = two.tile([P, 2, 1024], BF16, name="w_grouped", tag="w_grouped", align_bytes=64)
            for a in range(2):
                nc.scalar.copy(
                    grouped[:, a, :].rearrange("p (c i j) -> p c j i", i=4, j=4),
                    raw[:, a, :, :].rearrange("p j (c i) -> p c j i", i=4),
                )
            codes = keep.tile([P, BANK], U32, name="w_codes", tag=tag, align_bytes=64)
            scales = keep.tile([P, BANK], U8, name=f"w_scales{first_tile}", align_bytes=64)
            nc.vector.quantize_mx(codes[:].bitcast(FP8X4), scales[:], grouped[:].rearrange("p a n -> p (a n)"))
            for n in range(2):
                for a in range(2):
                    cols = slice(256 * a + P * n, 256 * a + P * (n + 1))
                    weights[first_tile + n, a] = (codes[:, cols], scales[:, cols])

        def quantise_w1_dealt(a, raw, codes, scales):
            grouped = two.tile([P, 4 * BANK], BF16, name="w_grouped", tag="w_grouped", align_bytes=64)
            nc.scalar.copy(
                grouped[:].rearrange("p (t m j) -> p m t j", t=4, j=4),
                raw[:].rearrange("p j (m t) -> p m t j", t=4),
            )
            nc.vector.quantize_mx(codes.bitcast(FP8X4), scales, grouped[:])
            for t in range(4):
                cols = slice(P * t, P * (t + 1))
                weights[4 + t, a] = (codes[:, cols], scales[:, cols])

        chains = {}
        pages = {}

        def load_chain(i):
            chains[i] = three.tile([P, S], F32, name="chain", tag="chain")
            nc.sync.dma_start(chains[i][:], tile_rows(chain, i))

        def load_page(i):
            pages[i] = four.tile([P, T2], F32, name="page", tag="page")
            nc.sync.dma_start(pages[i][:], tile_rows(page0, i))

        v_planes = zeroed_planes(S, "v_planes")
        ident = keep.tile([P, P], F32, name="ident")
        make_identity(nc, ident[:])
        v2_planes = zeroed_planes(S2, "v2_planes")
        sk_planes = zeroed_planes(NP, "sk_planes")

        tab_sc = scale_window(tab_scales, T, "tab_sc")
        idx = load_list(offs, "idx")
        raw_first = load_w1_pair(0)
        tab2_sc = scale_window(tab2_scales, T3, "tab2_sc")
        idx2 = load_list(offs2, "idx2")
        tab_w = [keep.tile([P, T], U32, name=f"tab_w{a}", tag=f"big{a}", align_bytes=64) for a in range(2)]
        load_words(tab_words[0], tab_w[0])

        v_sc = keep.tile([P, S], U8, name="v_sc", align_bytes=64)
        nc.vector.tensor_copy(v_sc[:], tab_sc[:].indirect(idx[:]))
        place_scales(v_planes, v_sc)
        load_words(tab_words[1], tab_w[1])

        chains[0] = three.tile([P, S], F32, name="chain", tag="chain")
        wgs_plain = keep.tile([P, S], F32, name="wgs_plain")
        nc.sync.dma_start(chains[0][:, :BANK], tile_rows(chain, 0)[:, :BANK])
        nc.sync.dma_start(wgs_plain[:, :BANK], wgs[:, :BANK])
        idx3 = load_list(offs3, "idx3")
        load_page(0)
        nc.sync.dma_start(chains[0][:, BANK:], tile_rows(chain, 0)[:, BANK:])
        nc.sync.dma_start(wgs_plain[:, BANK:], wgs[:, BANK:])
        load_chain(1)
        idx4 = load_list(offs4, "idx4")
        raw_second = load_w1_pair(256)
        load_page(1)
        load_chain(2)

        v2_sc = keep.tile([P, S2], U8, name="v2_sc", align_bytes=64)
        nc.vector.tensor_copy(v2_sc[:], tab2_sc[:].indirect(idx2[:]))
        quantise_w1_pair(raw_first, 0, "codes_first")
        v = [keep.tile([P, S], U32, name=f"v{a}", align_bytes=64) for a in range(2)]
        nc.vector.tensor_copy(v[0][:], tab_w[0][:].indirect(idx[:]))
        for hh in range(2):
            nc.vector.tensor_copy(
                v[1][:, BANK * hh : BANK * (hh + 1)],
                tab_w[1][:].indirect(idx[:, 32 * hh : 32 * (hh + 1)]),
            )

        hs = {}

        def make_h(i):
            h = keep.tile([P, S], F32, name=f"h{i}", tag="h" + "ABFCBDEC"[i], align_bytes=64)
            hs[i] = h
            for hh in range(2):
                cols = slice(BANK * hh, BANK * (hh + 1))
                acc = bank(hh if i not in ADD_ON_VECTOR else 6 + hh)
                for a in range(2):
                    codes, scales = weights[i, a]
                    nc.tensor.matmul_mx(
                        acc[:],
                        lhsT=codes.bitcast(FP8X4),
                        lhsT_scale=scales,
                        rhs=v[a][:, cols].bitcast(FP8X4),
                        rhs_scale=v_planes[:, a, cols],
                        start=(a == 0),
                        stop=(a == 1),
                    )
                if i in ADD_ON_VECTOR:
                    nc.vector.tensor_tensor(h[:, cols], acc[:], chains[i][:, cols], ADD)
                    continue
                plain = keep.tile([P, BANK], F32, name="plain", tag=f"plain{hh}", align_bytes=64)
                nc.scalar.copy(plain[:], acc[:])
                turned = bank(2 + hh)
                for n, src in enumerate((chains[i][:, cols], plain[:])):
                    for c in range(4):
                        blk = slice(P * c, P * (c + 1))
                        nc.tensor.matmul(
                            turned[:, blk], lhsT=src[:, blk], rhs=ident[:], is_transpose=True,
                            start=(n == 0 and c == 0), stop=(n == 1 and c == 3),
                        )
                summed = keep.tile([P, BANK], F32, name="summed", tag=f"summed{hh}", align_bytes=64)
                nc.scalar.copy(summed[:], turned[:])
                back = bank(4 + hh)
                for c in range(4):
                    blk = slice(P * c, P * (c + 1))
                    nc.tensor.transpose(back[:, blk], summed[:, blk], ident[:])
                nc.scalar.copy(h[:, cols], back[:])

        picked = {}

        def scatter(i, pieces=1):
            factors = wgs_plain[:] if i < 4 else wgs_dealt[:, i - 4, :]
            width = S // pieces
            for n in range(pieces):
                cols = slice(width * n, width * (n + 1))
                nc.vector.tensor_tensor(
                    pages[i][:].indirect(idx3[:, width // 16 * n : width // 16 * (n + 1)]),
                    hs[i][:, cols], factors[:, cols], MULT,
                )

        def fetch(i, pieces=1):
            picked[i] = keep.tile([P, NP], F32, name="picked", tag=f"picked{i % 4}")
            width = NP // pieces
            for n in range(pieces):
                nc.vector.tensor_copy(
                    picked[i][:, width * n : width * (n + 1)],
                    pages[i][:].indirect(idx4[:, width // 16 * n : width // 16 * (n + 1)]),
                )

        regrouped = keep.tile([P, 4, NP], F32, name="regrouped", tag="regrouped")

        def regroup(i):
            nc.sync.dma_start(regrouped[32 * i : 32 * (i + 1), :, :], picked[i][:])

        wgs_dealt = keep.tile([P, 4, S], F32, name="wgs_dealt")

        def load_wgs_dealt(t):
            rows = wgs.rearrange("(q t) j -> t q j", t=4)[t]
            for q in range(4):
                nc.sync.dma_start(wgs_dealt[32 * q : 32 * q + 32, t, :], rows)

        make_h(0)
        scatter(0, pieces=2)
        make_h(1)
        fetch(0)
        quantise_w1_pair(raw_second, 2, "hA")
        raw_dealt = [load_w1_dealt(0)]
        load_chain(3)
        load_page(2)
        raw_dealt.append(load_w1_dealt(1))
        load_chain(4)
        load_page(3)
        load_wgs_dealt(0)
        load_page(4)
        scatter(1)
        make_h(2)
        fetch(1)
        make_h(3)
        load_chain(5)
        load_chain(6)
        regroup(0)
        regroup(1)
        load_wgs_dealt(1)
        scatter(2)
        fetch(2)
        codes_dealt = keep.tile([P, 2, BANK], U32, name="codes_dealt", tag="hF", align_bytes=64)
        scales_dealt = keep.tile([P, 2, BANK], U8, name="scales_dealt", align_bytes=64)
        for a in range(2):
            quantise_w1_dealt(a, raw_dealt[a], codes_dealt[:, a, :], scales_dealt[:, a, :])
        make_h(4)
        load_chain(7)
        tab2_w = [two.tile([P, T3], U32, name="tab2_w", tag="raw", align_bytes=64) for a in range(2)]
        for a in range(2):
            load_words(tab2_words[a], tab2_w[a])
        place_scales(v2_planes, v2_sc)
        load_page(5)
        scatter(3)
        fetch(3)
        regroup(2)
        regroup(3)
        sk_w = keep.tile([P, 2, 2 * NP], U8, name="sk_w", align_bytes=64)
        nc.sync.dma_start(sk_w[:].bitcast(I32), sk_words.bitcast(I32).rearrange("a p n -> p a n"))
        for q in range(4):
            nc.sync.dma_start(
                sk_planes[32 * q : 32 * q + 4, :, :].bitcast(I32),
                sk_scales[:, 4 * q : 4 * q + 4, :].bitcast(I32).rearrange("a r n -> r a n"),
            )
        gains = keep.tile([P, 2, 4], F32, name="gains")
        nc.sync.dma_start(gains[:], gain.rearrange("(a p t) -> p a t", a=2, t=4))
        load_wgs_dealt(2)
        load_page(6)
        load_wgs_dealt(3)
        load_page(7)
        periods = keep.tile([P, 8, NP], F32, name="periods", tag="big0", align_bytes=64)
        nc.sync.dma_start(periods[:], period.rearrange("(m p) j -> p m j", p=P))
        make_h(5)
        scatter(4)
        fetch(4)
        v2 = [keep.tile([P, S2], U32, name=f"v2{a}", align_bytes=64) for a in range(2)]
        for a in range(2):
            nc.vector.tensor_copy(v2[a][:], tab2_w[a][:].indirect(idx2[:]))
        make_h(6)
        make_h(7)

        woven = [
            keep.tile([P, NP, 4], BF16, name="woven0", tag="summed1", align_bytes=64),
            keep.tile([P, NP, 4], BF16, name="woven1", tag="plain1", align_bytes=64),
        ]

        def weave(a, t, src, cols):
            nc.scalar.activation(woven[a][:, cols, t], src, COPY, scale=gains[:, a, t : t + 1])

        every = slice(0, NP)
        for t in range(4):
            weave(0, t, regrouped[:, t, :], every)

        sketch = keep.tile([P, 8, NP], F32, name="sketch", tag="big1", align_bytes=64)
        for m in range(8):
            rows = slice(P * m, P * (m + 1))
            acc = bank(m % 4)
            for a in range(2):
                nc.tensor.matmul_mx(
                    acc[:],
                    lhsT=v2[a][:, rows].bitcast(FP8X4),
                    lhsT_scale=v2_planes[:, a, rows],
                    rhs=sk_w[:, a, :].bitcast(FP4X4),
                    rhs_scale=sk_planes[:, a, :],
                    start=(a == 0),
                    stop=(a == 1),
                )
            nc.scalar.copy(sketch[:, m, :], acc[:])

        weave(1, 0, picked[4][:], every)
        for i in (5, 6):
            scatter(i)
            fetch(i)
            weave(1, i - 4, picked[i][:], every)

        x_codes = [
            keep.tile([P, NP], U32, name="x_codes0", tag="hE", align_bytes=64),
            keep.tile([P, NP], U32, name="x_codes1", align_bytes=64),
        ]
        x_scales = [keep.tile([P, NP], U8, name=f"x_scales{a}", align_bytes=64) for a in range(2)]
        nc.vector.quantize_mx(
            x_codes[0][:].bitcast(FP8X4), x_scales[0][:], woven[0][:].rearrange("p j t -> p (j t)")
        )

        half = NP // 2
        scores = {}

        def score_pass(hh, mp, a):
            cols = slice(half * hh, half * (hh + 1))
            for n in range(2):
                rows = slice(P * (2 * mp + n), P * (2 * mp + n + 1))
                nc.tensor.matmul_mx(
                    scores[hh, mp][:, half * n : half * (n + 1)],
                    lhsT=v2[a][:, rows].bitcast(FP8X4),
                    lhsT_scale=v2_planes[:, a, rows],
                    rhs=x_codes[a][:, cols].bitcast(FP8X4),
                    rhs_scale=x_scales[a][:, cols],
                    start=(a == 0 and n == 0),
                    stop=(a == 1 and n == 1),
                )

        for hh in range(2):
            for mp in range(4):
                scores[hh, mp] = bank(4 * hh + mp)
                score_pass(hh, mp, 0)

        scatter(7)
        fetch(7, pieces=2)

        out_rows = out.rearrange("(m p) j -> p m j", p=P)
        for hh in range(2):
            cols = slice(half * hh, half * (hh + 1))
            weave(1, 3, picked[7][:, cols], cols)
            nc.vector.quantize_mx(
                x_codes[1][:, cols].bitcast(FP8X4),
                x_scales[1][:, cols],
                woven[1][:, cols, :].rearrange("p j t -> p (j t)"),
            )
            for mp in range(4):
                score_pass(hh, mp, 1)
        chunks = [(hh, mp) for hh in range(2) for mp in range(4)]
        weighted = {}
        results = [four.tile([P, 8, half], F32, name="results", tag="page") for hh in range(2)]

        def weigh(hh, mp):
            cols = slice(half * hh, half * (hh + 1))
            bounded = three.tile([P, 2, half], F32, name="bounded", tag="bounded")
            nc.scalar.activation(bounded[:], scores[hh, mp][:].rearrange("p (n j) -> p n j", n=2), TANH)
            weighted[hh, mp] = three.tile([P, 2, half], F32, name="weighted", tag="weighted")
            nc.vector.tensor_tensor(weighted[hh, mp][:], bounded[:], periods[:, 2 * mp : 2 * mp + 2, cols], MULT)

        def finish(hh, mp):
            cols = slice(half * hh, half * (hh + 1))
            pair = slice(2 * mp, 2 * mp + 2)
            result = results[hh][:, pair, :]
            nc.vector.tensor_tensor(result, weighted[hh, mp][:], sketch[:, pair, cols], MAX)
            nc.sync.dma_start(out_rows[:, pair, cols], result)

        weigh(*chunks[0])
        for n in range(1, len(chunks)):
            weigh(*chunks[n])
            finish(*chunks[n - 1])
        finish(*chunks[-1])
